import numpy as np
import ml_dtypes


def mxq(x, axis, fmt="e4m3"):
    dtype, down = {"e4m3": (ml_dtypes.float8_e4m3fn, 7), "e5m2": (ml_dtypes.float8_e5m2, 14)}[fmt]
    v = np.moveaxis(np.asarray(x, np.float32).astype(ml_dtypes.bfloat16).astype(np.float64), axis, -1)
    blocks = v.reshape(v.shape[:-1] + (-1, 32))
    amax = np.abs(blocks).max(-1, keepdims=True)
    byte = np.maximum(np.where(amax > 0, np.frexp(amax)[1] - 1 + 127, 0) - down, 1)
    scale = np.exp2(byte - 127.0)
    codes = (blocks / scale).astype(np.float32).astype(dtype).astype(np.float64)
    return np.moveaxis((codes * scale).reshape(v.shape), -1, axis)


WIDE = False


def mx_kscale(k):
    if not WIDE:
        return np.ones(k)
    levels = np.array([10, -10, 5, -5, 0])
    if k % 512:
        return np.exp2(np.random.permutation(np.resize(levels, k // 32))).repeat(32)
    a = np.empty((k // 512, 16))
    for p in range(k // 512):
        a[p, :8] = np.random.permutation(np.resize(levels, 8))
        for g in range(8):
            far = levels[np.abs(levels - a[p, g]) >= 10]
            a[p, g + 8] = far[np.random.randint(len(far))]
    return np.exp2(a.ravel()).repeat(32)


def f64(x):
    return np.asarray(x).astype(np.float64)


def striped(idx):
    return np.tile(idx.reshape(-1, 16).T, (8, 1)).astype(np.uint16)


def unstriped(offs):
    return offs[:16].T.reshape(-1).astype(np.int64)


E2M1 = np.array([0.0, 0.5, 1.0, 1.5, 2.0, 3.0, 4.0, 6.0, -0.0, -0.5, -1.0, -1.5, -2.0, -3.0, -4.0, -6.0])


def pack_weight(w, fmt):
    k, n = w.shape
    w = f64(np.asarray(w, np.float32).astype(ml_dtypes.bfloat16)).reshape(k // 32, 32, n)
    amax = np.abs(w).max(1)
    if fmt == "e4m3":
        byte = np.frexp(amax)[1] - 1 + 127 - 7
    else:
        mant, ex = np.frexp(amax / 6.0)
        byte = np.where(mant > 0.5, ex, ex - 1) + 127
    byte = np.clip(np.where(amax > 0, byte, 1), 1, 254)
    scaled = (w * np.exp2(127.0 - byte)[:, None, :]).reshape(k, n).astype(np.float32)
    by_word = np.ascontiguousarray(scaled.reshape(k // 512, 128, 4, n).transpose(0, 1, 3, 2))
    if fmt == "e4m3":
        words = by_word.astype(ml_dtypes.float8_e4m3fn).view(np.uint8)
    else:
        c = by_word.astype(ml_dtypes.float4_e2m1fn).view(np.uint8) & 0xF
        words = (c[..., 0::2] | (c[..., 1::2] << 4)).reshape(k // 512, 128, 2 * n)
    return np.ascontiguousarray(words), np.ascontiguousarray(byte.astype(np.uint8).reshape(k // 512, 16, n))


def unpack_weight(words, scales, fmt):
    g, _, n = scales.shape
    words = np.ascontiguousarray(words).reshape(g, 128, n, -1)
    if fmt == "e4m3":
        vals = words.view(ml_dtypes.float8_e4m3fn).astype(np.float64)
    else:
        nib = np.empty((g, 128, n, 4), np.uint8)
        nib[..., 0::2] = words & 0xF
        nib[..., 1::2] = words >> 4
        vals = E2M1[nib]
    vals = vals * np.repeat(np.exp2(scales.astype(np.float64) - 127.0), 8, axis=1)[..., None]
    return vals.transpose(0, 1, 3, 2).reshape(g * 512, n)


def gelu(v):
    return 0.5 * v * (1.0 + np.tanh(np.sqrt(2.0 / np.pi) * (v + 0.044715 * v**3)))


def bf(x):
    return np.asarray(x, np.float32).astype(ml_dtypes.bfloat16)


def planes(Y):
    n, m = Y.shape
    b = f64(bf(Y)).reshape(n // 32, 32, m)
    amax = np.abs(b).max(1)
    byte = np.clip(np.where(amax > 0, np.frexp(amax)[1] - 1 + 127 - 7, 1), 1, 254)
    codes = (b * np.exp2(127.0 - byte)[:, None, :]).reshape(n, m).astype(np.float32).astype(ml_dtypes.float8_e4m3fn).view(np.uint8)
    words = codes.reshape(n // 512, 128, 4, m).transpose(0, 1, 3, 2)
    return np.ascontiguousarray(words), np.ascontiguousarray(byte.astype(np.uint8).reshape(n // 512, 16, m))


K, H, N, T, S, P = 1024, 512, 1024, 4096, 1024, 512

def setup_inputs():
    n = np.random.standard_normal
    s = mx_kscale(K)[:, None]
    u = mx_kscale(H)[:, None]
    size = np.exp(0.8 * n(N))[None, :]
    visits = np.random.permutation(S)
    d = {}
    d["tab_words"], d["tab_scales"] = pack_weight(n((K, T)) * s, "e4m3")
    d["offs"] = striped(np.random.permutation(T)[:S])
    d["pos1"] = striped(visits[:P])
    d["pos2"] = striped(visits[P:2 * P])
    d["wa"] = (1.2 * n((K, H)) / s / K ** 0.5).astype(np.float32)
    d["wb_words"], d["wb_scales"] = pack_weight(1.6 * n((K, H)) / s / K ** 0.5, "e2m1")
    d["gain"] = (np.exp(0.3 * n(H)) * u[:, 0]).astype(np.float32)
    d["wc"] = (n((H, N)) * size / u / H ** 0.5).astype(np.float32)
    d["wd_words"], d["wd_scales"] = pack_weight(n((H, N)) * size / u / H ** 0.5, "e4m3")
    return d

def reference(tab_words, tab_scales, offs, pos1, pos2, wa, wb_words, wb_scales, gain, wc, wd_words, wd_scales):
    v = unpack_weight(tab_words, tab_scales, "e4m3")[:, unstriped(offs)]
    wb = unpack_weight(wb_words, wb_scales, "e2m1")
    wd = unpack_weight(wd_words, wd_scales, "e4m3")
    a = mxq(f64(wa), 0, "e4m3").T @ v
    b = wb.T @ v
    h = f64(gain)[:, None] * (np.exp(-np.abs(a)) * b)
    hq = mxq(h, 0, "e4m3")
    dark = mxq(f64(wc), 0, "e4m3").T @ hq
    tint = wd.T @ hq
    ink = np.maximum(dark, tint)
    y = ink[:, unstriped(pos1)] - ink[:, unstriped(pos2)]
    words, scales = planes(y)
    return y, words, scales

@@ -1,0 +1,329 @@
+from contextlib import ExitStack
+
+import concourse.mybir as mybir
+
+K, H, N, T, S, PAIRS = 1024, 512, 1024, 4096, 1024, 512
+FLOPS = 2 * 2 * K * H * S + 2 * 2 * H * N * S
+
+F32 = mybir.dt.float32
+BF16 = mybir.dt.bfloat16
+I32 = mybir.dt.int32
+U32 = mybir.dt.uint32
+U16 = mybir.dt.uint16
+U8 = mybir.dt.uint8
+FP8X4 = mybir.dt.float8_e4m3fn_x4
+FP4X4 = mybir.dt.float4_e2m1fn_x4
+ALU = mybir.AluOpType
+ACT = mybir.ActivationFunctionType
+
+P = 128
+PACK = 4
+BANK = 512
+CHUNK = 256
+
+
+def tile_list_tattoo_fading_score_kernel(
+    tc, tab_words, tab_scales, offs, pos1, pos2, wa, wb_words, wb_scales, gain, wc, wd_words, wd_scales, out_0, out_1, out_2
+):
+    nc = tc.nc
+    with ExitStack() as ctx:
+        keep = ctx.enter_context(tc.tile_pool(name="keep", bufs=1))
+        ring = ctx.enter_context(tc.tile_pool(name="ring", bufs=3))
+        psum = ctx.enter_context(tc.psum_pool(name="psum", bufs=4))
+
+        def held(shape, dtype, name):
+            return keep.tile(shape, dtype, name=name, align_bytes=64)
+
+        offs_sb = keep.tile([P, S // 16], U16, name="offs_sb")
+        pos1_sb = keep.tile([P, PAIRS // 16], U16, name="pos1_sb")
+        pos2_sb = keep.tile([P, PAIRS // 16], U16, name="pos2_sb")
+        tab_sb = [held([P, T], U32, "tab_sb%d" % a) for a in range(2)]
+        tabsc_raw = held([P, T], U8, "tabsc_raw")
+        tabsc_picked = held([P, S], U8, "tabsc_picked")
+        staged = held([P, S + 2 * BANK], U8, "staged")
+        planes = held([P, 2, S + 2 * BANK], U8, "planes")
+        v_words = [held([P, S], U32, "v_words%d" % a) for a in range(2)]
+        wb_raw = held([P, 2, 2 * H], U8, "wb_raw")
+        wb_dealt = held([P, 2, 2 * H], U8, "wb_dealt")
+        wsc_raw = held([P, 2, BANK], U8, "wsc_raw")
+        wd_raw = held([P, N], U32, "wd_raw")
+        wd_dealt = held([P, N], U32, "wd_dealt")
+        gain_sb = held([P, PACK], F32, "gain_sb")
+        wa_raw = [held([P, PACK, H], F32, "wa_raw%d" % a) for a in range(2)]
+        wc_raw = [held([P, PACK, BANK], F32, "wc_raw%d" % g) for g in range(2)]
+        wa_codes = [held([P, H], U32, "wa_codes%d" % a) for a in range(2)]
+        wa_scales = [held([P, H], U8, "wa_scales%d" % a) for a in range(2)]
+        wc_codes = [held([P, BANK], U32, "wc_codes%d" % g) for g in range(2)]
+        wc_scales = [held([P, BANK], U8, "wc_scales%d" % g) for g in range(2)]
+        h_codes = held([P, S], U32, "h_codes")
+        h_scales = held([P, S], U8, "h_scales")
+        warm = held([P, 8], F32, "warm")
+
+        nc.sync.dma_start(offs_sb[:], offs)
+        nc.sync.dma_start(tabsc_raw[0:32, :].bitcast(I32), tab_scales.rearrange("a q t -> (a q) t").bitcast(I32))
+        nc.sync.dma_start(wsc_raw[0:32, 0, :].bitcast(I32), wb_scales.rearrange("a q c -> (a q) c").bitcast(I32))
+        for g in range(2):
+            nc.sync.dma_start(
+                wsc_raw[16 * g : 16 * (g + 1), 1, :].bitcast(I32),
+                wd_scales[0, :, BANK * g : BANK * (g + 1)].bitcast(I32),
+            )
+        for lo, hi in ((32, 64), (64, P)):
+            nc.vector.memset(tabsc_raw[lo:hi, :].bitcast(I32), 0)
+            nc.vector.memset(wsc_raw[lo:hi, :, :].rearrange("p a c -> p (a c)").bitcast(I32), 0)
+        nc.vector.memset(planes[:].rearrange("p a c -> p (a c)").bitcast(I32), 0)
+        nc.vector.memset(warm[:], 0.0)
+        nc.scalar.activation(warm[:, 4:5], warm[:, 0:1], ACT.Exp)
+
+        def load_table(a):
+            nc.sync.dma_start(tab_sb[a][:].bitcast(I32), tab_words[a].rearrange("p t i -> p (t i)").bitcast(I32))
+
+        load_table(0)
+        nc.sync.dma_start(wb_raw[:].bitcast(I32), wb_words.rearrange("a p c -> p a c").bitcast(I32))
+        nc.sync.dma_start(gain_sb[:], gain.rearrange("(p t) -> p t", t=PACK))
+        load_table(1)
+        for a in range(2):
+            nc.sync.dma_start(wa_raw[a][:], wa[512 * a : 512 * (a + 1), :].rearrange("(p j) c -> p j c", j=PACK))
+
+        def load_wc(g):
+            nc.sync.dma_start(wc_raw[g][:], wc[:, BANK * g : BANK * (g + 1)].rearrange("(p j) c -> p j c", j=PACK))
+
+        load_wc(0)
+        nc.sync.dma_start(wd_raw[:].bitcast(I32), wd_words[0].rearrange("p c i -> p (c i)").bitcast(I32))
+        load_wc(1)
+        nc.sync.dma_start(pos1_sb[:], pos1)
+        nc.sync.dma_start(pos2_sb[:], pos2)
+
+        nc.vector.tensor_copy(
+            staged[:, S:].rearrange("p (w t m) -> p w m t", w=2, t=PACK),
+            wsc_raw[:].rearrange("p w (m t) -> p w m t", t=PACK),
+        )
+        nc.vector.tensor_copy(tabsc_picked[:], tabsc_raw[:].indirect(offs_sb[:]))
+        nc.vector.tensor_copy(staged[0:32, 0:S].bitcast(I32), tabsc_picked[0:32, :].bitcast(I32))
+        for a in range(2):
+            for q in range(4):
+                first = 16 * a + 4 * q
+                nc.gpsimd.dma_start(
+                    planes[32 * q : 32 * q + 4, a, :].bitcast(I32), staged[first : first + 4, :].bitcast(I32)
+                )
+        nc.vector.tensor_copy(
+            wb_dealt[:].rearrange("p a (t m b) -> p a m t b", t=PACK, b=2),
+            wb_raw[:].rearrange("p a (m t b) -> p a m t b", t=PACK, b=2),
+        )
+        nc.vector.tensor_copy(v_words[0][:], tab_sb[0][:].indirect(offs_sb[:]))
+        for hf in range(2):
+            nc.vector.tensor_copy(
+                v_words[1][:, BANK * hf : BANK * (hf + 1)],
+                tab_sb[1][:].indirect(offs_sb[:, 32 * hf : 32 * (hf + 1)]),
+            )
+
+        bg = [held([P, PACK, BANK], F32, "bg%d" % hf) for hf in range(2)]
+        for hf in range(2):
+            cols = slice(BANK * hf, BANK * (hf + 1))
+            banks = [psum.tile([P, BANK], F32, name="pb", tag="pb") for t in range(PACK)]
+            for a in range(2):
+                for t in range(PACK):
+                    nc.tensor.matmul_mx(
+                        out=banks[t][:],
+                        lhsT=wb_dealt[:, a, 2 * P * t : 2 * P * (t + 1)].bitcast(FP4X4),
+                        lhsT_scale=planes[:, a, S + P * t : S + P * (t + 1)],
+                        rhs=v_words[a][:, cols].bitcast(FP8X4),
+                        rhs_scale=planes[:, a, cols],
+                        start=(a == 0),
+                        stop=(a == 1),
+                    )
+            for t in range(PACK):
+                nc.scalar.activation(bg[hf][:, t, :], banks[t][:], ACT.Copy, scale=gain_sb[:, t : t + 1])
+
+        def round_and_deal(copy, raw, first, count, name):
+            if name == "wc_bf1":
+                dealt = ring.tile([P, count, P, PACK], BF16, name=name, tag="size", bufs=2, align_bytes=64)
+            else:
+                dealt = held([P, count, P, PACK], BF16, name)
+            copy(
+                dealt[:].rearrange("p t m j -> p m j t"),
+                raw[:].rearrange("p j (m t) -> p m j t", t=PACK)[:, :, :, first : first + count],
+            )
+            return dealt
+
+        def quantise(dealt, codes, scales):
+            nc.vector.quantize_mx(out=codes.bitcast(FP8X4), scales=scales, in_=dealt)
+
+        def quantise_weight(dealt, codes, scales, first, count):
+            cols = slice(P * first, P * (first + count))
+            quantise(dealt[:].rearrange("p t m j -> p (t m j)"), codes[:, cols], scales[:, cols])
+
+        def a_passes(bank, c, pair, a):
+            cols = slice(CHUNK * c, CHUNK * (c + 1))
+            for i in range(2):
+                t = 2 * pair + i
+                nc.tensor.matmul_mx(
+                    out=bank[:, CHUNK * i : CHUNK * (i + 1)],
+                    lhsT=wa_codes[a][:, P * t : P * (t + 1)].bitcast(FP8X4),
+                    lhsT_scale=wa_scales[a][:, P * t : P * (t + 1)],
+                    rhs=v_words[a][:, cols].bitcast(FP8X4),
+                    rhs_scale=planes[:, a, cols],
+                    start=(a == 0 and i == 0),
+                    stop=(a == 1 and i == 1),
+                )
+
+        wa0 = round_and_deal(nc.vector.tensor_copy, wa_raw[0], 0, PACK, "wa_bf0")
+        quantise_weight(wa0, wa_codes[0], wa_scales[0], 0, PACK)
+        a_banks = {}
+        for c in range(2):
+            for pair in range(2):
+                a_banks[c, pair] = psum.tile([P, BANK], F32, name="pa", tag="pa")
+                a_passes(a_banks[c, pair], c, pair, 0)
+        wa1 = [round_and_deal(nc.vector.tensor_copy, wa_raw[1], 2 * pair, 2, "wa_bf1%d" % pair) for pair in range(2)]
+        for pair in range(2):
+            quantise_weight(wa1[pair], wa_codes[1], wa_scales[1], 2 * pair, 2)
+
+        damp = {}
+
+        def damping(c):
+            size = ring.tile([P, PACK, CHUNK], F32, name="size", bufs=2, align_bytes=64)
+            for pair in range(2):
+                if (c, pair) not in a_banks:
+                    a_banks[c, pair] = psum.tile([P, BANK], F32, name="pa", tag="pa")
+                    a_passes(a_banks[c, pair], c, pair, 0)
+                a_passes(a_banks[c, pair], c, pair, 1)
+                nc.scalar.activation(
+                    size[:, 2 * pair : 2 * pair + 2, :].rearrange("p t m -> p (t m)"), a_banks[c, pair][:], ACT.Abs
+                )
+            damp[c] = ring.tile([P, PACK, CHUNK], F32, name="damp", align_bytes=64)
+            nc.scalar.activation(
+                damp[c][:].rearrange("p t m -> p (t m)"), size[:].rearrange("p t m -> p (t m)"), ACT.Exp, scale=-1.0
+            )
+
+        h_bf = {}
+
+        def features(c):
+            h_bf[c] = ring.tile([P, CHUNK, PACK], BF16, name="h_bf", align_bytes=64)
+            lo = CHUNK * (c % 2)
+            nc.vector.tensor_tensor(
+                h_bf[c][:].rearrange("p (c i) t -> p c t i", i=4),
+                damp[c][:].rearrange("p t (c i) -> p c t i", i=4),
+                bg[c // 2][:, :, lo : lo + CHUNK].rearrange("p t (c i) -> p c t i", i=4),
+                ALU.mult,
+            )
+
+        def quantise_h(c):
+            cols = slice(CHUNK * c, CHUNK * (c + 1))
+            quantise(h_bf[c][:].rearrange("p m t -> p (m t)"), h_codes[:, cols], h_scales[:, cols])
+
+        for c in range(4):
+            damping(c)
+        wc0 = round_and_deal(nc.vector.tensor_copy, wc_raw[0], 0, PACK, "wc_bf0")
+        features(0)
+        quantise_weight(wc0, wc_codes[0], wc_scales[0], 0, PACK)
+        quantise_h(0)
+        nc.vector.tensor_copy(
+            wd_dealt[:].bitcast(I32).rearrange("p (g t m) -> p g m t", g=2, t=PACK),
+            wd_raw[:].bitcast(I32).rearrange("p (g m t) -> p g m t", g=2, t=PACK),
+        )
+        features(1)
+        quantise_h(1)
+        features(2)
+        quantise_h(2)
+        features(3)
+        quantise_h(3)
+
+        ink = {}
+        y = [held([P, PACK, PAIRS], F32, "y%d" % g) for g in range(2)]
+        y_codes = [held([P, PAIRS], U32, "y_codes%d" % g) for g in range(2)]
+        y_scales = [held([P, PAIRS], U8, "y_scales%d" % g) for g in range(2)]
+
+        def scores(i, hf):
+            g, t = divmod(i, PACK)
+            if hf == 0:
+                ink[i] = ring.tile([P, S], F32, name="ink", bufs=4, align_bytes=64)
+            cols = slice(BANK * hf, BANK * (hf + 1))
+            dark = psum.tile([P, BANK], F32, name="pa", tag="pa")
+            nc.tensor.matmul_mx(
+                out=dark[:],
+                lhsT=wc_codes[g][:, P * t : P * (t + 1)].bitcast(FP8X4),
+                lhsT_scale=wc_scales[g][:, P * t : P * (t + 1)],
+                rhs=h_codes[:, cols].bitcast(FP8X4),
+                rhs_scale=h_scales[:, cols],
+                start=True,
+                stop=True,
+            )
+            tint = psum.tile([P, BANK], F32, name="pb", tag="pb")
+            nc.tensor.matmul_mx(
+                out=tint[:],
+                lhsT=wd_dealt[:, P * i : P * (i + 1)].bitcast(FP8X4),
+                lhsT_scale=planes[:, g, S + BANK + P * t : S + BANK + P * (t + 1)],
+                rhs=h_codes[:, cols].bitcast(FP8X4),
+                rhs_scale=h_scales[:, cols],
+                start=True,
+                stop=True,
+            )
+            dark_sb = ring.tile([P, BANK], F32, name="dark_sb", bufs=4, align_bytes=64)
+            nc.scalar.copy(dark_sb[:], dark[:])
+            nc.vector.tensor_tensor(ink[i][:, cols], tint[:], dark_sb[:], ALU.max)
+
+        later = {}
+
+        def pick_later(i, lo, hi):
+            later[i, lo] = ring.tile([P, hi - lo], F32, name="later", align_bytes=64)
+            nc.vector.tensor_copy(later[i, lo][:], ink[i][:].indirect(pos2_sb[:, lo // 16 : hi // 16]))
+
+        def difference(i, lo, hi):
+            g, t = divmod(i, PACK)
+            nc.vector.tensor_tensor(
+                y[g][:, t, lo:hi], ink[i][:].indirect(pos1_sb[:, lo // 16 : hi // 16]), later[i, lo][:], ALU.subtract
+            )
+            rows = out_0[512 * g : 512 * (g + 1), :].rearrange("(p t) j -> p t j", t=PACK)
+            nc.sync.dma_start(rows[:, t, lo:hi], y[g][:, t, lo:hi])
+
+        y_bf = {}
+
+        def round_y(copy, g, hf):
+            y_bf[g, hf] = held([P, CHUNK, PACK], BF16, "y_bf%d%d" % (g, hf))
+            copy(
+                y_bf[g, hf][:].rearrange("p (c i) t -> p c t i", i=4),
+                y[g][:, :, CHUNK * hf : CHUNK * (hf + 1)].rearrange("p t (c i) -> p c t i", i=4),
+            )
+
+        def quantise_y(g, hf):
+            cols = slice(CHUNK * hf, CHUNK * (hf + 1))
+            quantise(y_bf[g, hf][:].rearrange("p m t -> p (m t)"), y_codes[g][:, cols], y_scales[g][:, cols])
+            words = out_1[g].rearrange("p m t -> p (m t)").bitcast(I32)
+            nc.sync.dma_start(words[:, cols], y_codes[g][:, cols].bitcast(I32))
+
+        def store_scales(g):
+            for q in range(4):
+                queue = nc.scalar if q % 2 else nc.sync
+                queue.dma_start(
+                    out_2[g, 4 * q : 4 * q + 4, :].bitcast(I32), y_scales[g][32 * q : 32 * q + 4, :].bitcast(I32)
+                )
+
+        halves = [(i, 0) for i in range(3)] + [(i, 1) for i in range(3)]
+        halves = halves + [(i, hf) for i in range(3, 8) for hf in range(2)]
+        for i, hf in halves[:4]:
+            scores(i, hf)
+        wc1 = round_and_deal(nc.scalar.copy, wc_raw[1], 0, PACK, "wc_bf1")
+        for i in range(6):
+            scores(*halves[4 + 2 * i])
+            pick_later(i, 0, PAIRS)
+            if i == 1:
+                quantise_weight(wc1, wc_codes[1], wc_scales[1], 0, PACK)
+            scores(*halves[5 + 2 * i])
+            difference(i, 0, PAIRS)
+            if i == 3:
+                round_y(nc.scalar.copy, 0, 0)
+                round_y(nc.scalar.copy, 0, 1)
+            if i == 5:
+                quantise_y(0, 0)
+                quantise_y(0, 1)
+                store_scales(0)
+        pick_later(6, 0, PAIRS)
+        pick_later(7, 0, CHUNK)
+        difference(6, 0, PAIRS)
+        pick_later(7, CHUNK, PAIRS)
+        difference(7, 0, CHUNK)
+        round_y(nc.scalar.copy, 1, 0)
+        difference(7, CHUNK, PAIRS)
+        round_y(nc.vector.tensor_copy, 1, 1)
+        quantise_y(1, 0)
+        quantise_y(1, 1)
+        store_scales(1)

@@ -29,7 +29,7 @@ def tile_list_tattoo_fading_score_kernel(
     with ExitStack() as ctx:
         keep = ctx.enter_context(tc.tile_pool(name="keep", bufs=1))
         ring = ctx.enter_context(tc.tile_pool(name="ring", bufs=3))
-        psum = ctx.enter_context(tc.psum_pool(name="psum", bufs=4))
+        psum = ctx.enter_context(tc.psum_pool(name="psum", bufs=8))
 
         def held(shape, dtype, name):
             return keep.tile(shape, dtype, name=name, align_bytes=64)
@@ -60,13 +60,9 @@ def tile_list_tattoo_fading_score_kernel(
         warm = held([P, 8], F32, "warm")
 
         nc.sync.dma_start(offs_sb[:], offs)
-        nc.sync.dma_start(tabsc_raw[0:32, :].bitcast(I32), tab_scales.rearrange("a q t -> (a q) t").bitcast(I32))
-        nc.sync.dma_start(wsc_raw[0:32, 0, :].bitcast(I32), wb_scales.rearrange("a q c -> (a q) c").bitcast(I32))
-        for g in range(2):
-            nc.sync.dma_start(
-                wsc_raw[16 * g : 16 * (g + 1), 1, :].bitcast(I32),
-                wd_scales[0, :, BANK * g : BANK * (g + 1)].bitcast(I32),
-            )
+        nc.sync.dma_start(tabsc_raw[0:32, :].bitcast(I32), tab_scales.rearrange("a q t -> q a t").bitcast(I32))
+        nc.sync.dma_start(wsc_raw[0:32, 0, :].bitcast(I32), wb_scales.rearrange("a q c -> q a c").bitcast(I32))
+        nc.sync.dma_start(wsc_raw[0:32, 1, :].bitcast(I32), wd_scales[0].rearrange("q (g c) -> (q g) c", g=2).bitcast(I32))
         for lo, hi in ((32, 64), (64, P)):
             nc.vector.memset(tabsc_raw[lo:hi, :].bitcast(I32), 0)
             nc.vector.memset(wsc_raw[lo:hi, :, :].rearrange("p a c -> p (a c)").bitcast(I32), 0)
@@ -74,13 +70,30 @@ def tile_list_tattoo_fading_score_kernel(
         nc.vector.memset(warm[:], 0.0)
         nc.scalar.activation(warm[:, 4:5], warm[:, 0:1], ACT.Exp)
 
-        def load_table(a):
-            nc.sync.dma_start(tab_sb[a][:].bitcast(I32), tab_words[a].rearrange("p t i -> p (t i)").bitcast(I32))
+        def load_table(a, lo, hi):
+            words = tab_words[a].rearrange("p t i -> p (t i)").bitcast(I32)
+            nc.sync.dma_start(tab_sb[a][:, lo:hi].bitcast(I32), words[:, lo:hi])
 
-        load_table(0)
-        nc.sync.dma_start(wb_raw[:].bitcast(I32), wb_words.rearrange("a p c -> p a c").bitcast(I32))
+        nc.sync.dma_start(wb_raw[:, 0, :].bitcast(I32), wb_words[0].bitcast(I32))
+        load_table(0, 0, T)
         nc.sync.dma_start(gain_sb[:], gain.rearrange("(p t) -> p t", t=PACK))
-        load_table(1)
+        nc.sync.dma_start(pos1_sb[:], pos1)
+        nc.sync.dma_start(pos2_sb[:], pos2)
+        nc.sync.dma_start(wb_raw[:, 1, :].bitcast(I32), wb_words[1].bitcast(I32))
+        for i in range(4):
+            load_table(1, i * T // 8, (i + 1) * T // 8)
+
+        nc.vector.tensor_copy(
+            staged[:, S:].rearrange("p (w t m) -> p w t m", w=2, t=PACK),
+            wsc_raw[:].rearrange("p w (m t) -> p w t m", t=PACK),
+        )
+        nc.vector.tensor_copy(tabsc_picked[:], tabsc_raw[:].indirect(offs_sb[:]))
+        nc.vector.tensor_copy(staged[0:32, 0:S].bitcast(I32), tabsc_picked[0:32, :].bitcast(I32))
+        for q in range(4):
+            nc.sync.dma_start(
+                planes[32 * q : 32 * q + 4, :, :].bitcast(I32), staged[8 * q : 8 * q + 8, :].bitcast(I32)
+            )
+        load_table(1, T // 2, T)
         for a in range(2):
             nc.sync.dma_start(wa_raw[a][:], wa[512 * a : 512 * (a + 1), :].rearrange("(p j) c -> p j c", j=PACK))
 
@@ -90,26 +103,16 @@ def tile_list_tattoo_fading_score_kernel(
         load_wc(0)
         nc.sync.dma_start(wd_raw[:].bitcast(I32), wd_words[0].rearrange("p c i -> p (c i)").bitcast(I32))
         load_wc(1)
-        nc.sync.dma_start(pos1_sb[:], pos1)
-        nc.sync.dma_start(pos2_sb[:], pos2)
 
-        nc.vector.tensor_copy(
-            staged[:, S:].rearrange("p (w t m) -> p w m t", w=2, t=PACK),
-            wsc_raw[:].rearrange("p w (m t) -> p w m t", t=PACK),
-        )
-        nc.vector.tensor_copy(tabsc_picked[:], tabsc_raw[:].indirect(offs_sb[:]))
-        nc.vector.tensor_copy(staged[0:32, 0:S].bitcast(I32), tabsc_picked[0:32, :].bitcast(I32))
-        for a in range(2):
-            for q in range(4):
-                first = 16 * a + 4 * q
-                nc.gpsimd.dma_start(
-                    planes[32 * q : 32 * q + 4, a, :].bitcast(I32), staged[first : first + 4, :].bitcast(I32)
-                )
-        nc.vector.tensor_copy(
-            wb_dealt[:].rearrange("p a (t m b) -> p a m t b", t=PACK, b=2),
-            wb_raw[:].rearrange("p a (m t b) -> p a m t b", t=PACK, b=2),
-        )
+        def deal_wb(a):
+            nc.vector.tensor_copy(
+                wb_dealt[:, a, :].bitcast(U16).rearrange("p (t m) -> p t m", t=PACK),
+                wb_raw[:, a, :].bitcast(U16).rearrange("p (m t) -> p t m", t=PACK),
+            )
+
+        deal_wb(0)
         nc.vector.tensor_copy(v_words[0][:], tab_sb[0][:].indirect(offs_sb[:]))
+        deal_wb(1)
         for hf in range(2):
             nc.vector.tensor_copy(
                 v_words[1][:, BANK * hf : BANK * (hf + 1)],
@@ -117,13 +120,13 @@ def tile_list_tattoo_fading_score_kernel(
             )
 
         bg = [held([P, PACK, BANK], F32, "bg%d" % hf) for hf in range(2)]
-        for hf in range(2):
-            cols = slice(BANK * hf, BANK * (hf + 1))
-            banks = [psum.tile([P, BANK], F32, name="pb", tag="pb") for t in range(PACK)]
-            for a in range(2):
+        b_banks = [[psum.tile([P, BANK], F32, name="bank") for t in range(PACK)] for hf in range(2)]
+        for a in range(2):
+            for hf in range(2):
+                cols = slice(BANK * hf, BANK * (hf + 1))
                 for t in range(PACK):
                     nc.tensor.matmul_mx(
-                        out=banks[t][:],
+                        out=b_banks[hf][t][:],
                         lhsT=wb_dealt[:, a, 2 * P * t : 2 * P * (t + 1)].bitcast(FP4X4),
                         lhsT_scale=planes[:, a, S + P * t : S + P * (t + 1)],
                         rhs=v_words[a][:, cols].bitcast(FP8X4),
@@ -131,8 +134,9 @@ def tile_list_tattoo_fading_score_kernel(
                         start=(a == 0),
                         stop=(a == 1),
                     )
-            for t in range(PACK):
-                nc.scalar.activation(bg[hf][:, t, :], banks[t][:], ACT.Copy, scale=gain_sb[:, t : t + 1])
+        for hf in range(2):
+            for t in range(PACK - 2 * hf):
+                nc.scalar.activation(bg[hf][:, t, :], b_banks[hf][t][:], ACT.Copy, scale=gain_sb[:, t : t + 1])
 
         def round_and_deal(copy, raw, first, count, name):
             if name == "wc_bf1":
@@ -140,8 +144,8 @@ def tile_list_tattoo_fading_score_kernel(
             else:
                 dealt = held([P, count, P, PACK], BF16, name)
             copy(
-                dealt[:].rearrange("p t m j -> p m j t"),
-                raw[:].rearrange("p j (m t) -> p m j t", t=PACK)[:, :, :, first : first + count],
+                dealt[:].rearrange("p (u e) m j -> p u m j e", e=2),
+                raw[:].rearrange("p j (m u e) -> p u m j e", u=2, e=2)[:, first // 2 : (first + count) // 2, :, :, :],
             )
             return dealt
 
@@ -171,11 +175,11 @@ def tile_list_tattoo_fading_score_kernel(
         a_banks = {}
         for c in range(2):
             for pair in range(2):
-                a_banks[c, pair] = psum.tile([P, BANK], F32, name="pa", tag="pa")
+                a_banks[c, pair] = psum.tile([P, BANK], F32, name="bank")
                 a_passes(a_banks[c, pair], c, pair, 0)
-        wa1 = [round_and_deal(nc.vector.tensor_copy, wa_raw[1], 2 * pair, 2, "wa_bf1%d" % pair) for pair in range(2)]
         for pair in range(2):
-            quantise_weight(wa1[pair], wa_codes[1], wa_scales[1], 2 * pair, 2)
+            wa1 = round_and_deal(nc.vector.tensor_copy, wa_raw[1], 2 * pair, 2, "wa_bf1%d" % pair)
+            quantise_weight(wa1, wa_codes[1], wa_scales[1], 2 * pair, 2)
 
         damp = {}
 
@@ -183,13 +187,13 @@ def tile_list_tattoo_fading_score_kernel(
             size = ring.tile([P, PACK, CHUNK], F32, name="size", bufs=2, align_bytes=64)
             for pair in range(2):
                 if (c, pair) not in a_banks:
-                    a_banks[c, pair] = psum.tile([P, BANK], F32, name="pa", tag="pa")
+                    a_banks[c, pair] = psum.tile([P, BANK], F32, name="bank")
                     a_passes(a_banks[c, pair], c, pair, 0)
                 a_passes(a_banks[c, pair], c, pair, 1)
                 nc.scalar.activation(
                     size[:, 2 * pair : 2 * pair + 2, :].rearrange("p t m -> p (t m)"), a_banks[c, pair][:], ACT.Abs
                 )
-            damp[c] = ring.tile([P, PACK, CHUNK], F32, name="damp", align_bytes=64)
+            damp[c] = ring.tile([P, PACK, CHUNK], F32, name="damp", bufs=2, align_bytes=64)
             nc.scalar.activation(
                 damp[c][:].rearrange("p t m -> p (t m)"), size[:].rearrange("p t m -> p (t m)"), ACT.Exp, scale=-1.0
             )
@@ -200,9 +204,9 @@ def tile_list_tattoo_fading_score_kernel(
             h_bf[c] = ring.tile([P, CHUNK, PACK], BF16, name="h_bf", align_bytes=64)
             lo = CHUNK * (c % 2)
             nc.vector.tensor_tensor(
-                h_bf[c][:].rearrange("p (c i) t -> p c t i", i=4),
-                damp[c][:].rearrange("p t (c i) -> p c t i", i=4),
-                bg[c // 2][:, :, lo : lo + CHUNK].rearrange("p t (c i) -> p c t i", i=4),
+                h_bf[c][:].rearrange("p (c i) t -> p c t i", i=2),
+                damp[c][:].rearrange("p t (c i) -> p c t i", i=2),
+                bg[c // 2][:, :, lo : lo + CHUNK].rearrange("p t (c i) -> p c t i", i=2),
                 ALU.mult,
             )
 
@@ -216,9 +220,11 @@ def tile_list_tattoo_fading_score_kernel(
         features(0)
         quantise_weight(wc0, wc_codes[0], wc_scales[0], 0, PACK)
         quantise_h(0)
+        for t in range(2, PACK):
+            nc.vector.tensor_scalar_mul(bg[1][:, t, :], b_banks[1][t][:], gain_sb[:, t : t + 1])
         nc.vector.tensor_copy(
-            wd_dealt[:].bitcast(I32).rearrange("p (g t m) -> p g m t", g=2, t=PACK),
-            wd_raw[:].bitcast(I32).rearrange("p (g m t) -> p g m t", g=2, t=PACK),
+            wd_dealt[:].bitcast(I32).rearrange("p (g u e m) -> p g u m e", g=2, u=2, e=2),
+            wd_raw[:].bitcast(I32).rearrange("p (g m u e) -> p g u m e", g=2, u=2, e=2),
         )
         features(1)
         quantise_h(1)
@@ -237,7 +243,7 @@ def tile_list_tattoo_fading_score_kernel(
             if hf == 0:
                 ink[i] = ring.tile([P, S], F32, name="ink", bufs=4, align_bytes=64)
             cols = slice(BANK * hf, BANK * (hf + 1))
-            dark = psum.tile([P, BANK], F32, name="pa", tag="pa")
+            dark = psum.tile([P, BANK], F32, name="bank")
             nc.tensor.matmul_mx(
                 out=dark[:],
                 lhsT=wc_codes[g][:, P * t : P * (t + 1)].bitcast(FP8X4),
@@ -247,7 +253,7 @@ def tile_list_tattoo_fading_score_kernel(
                 start=True,
                 stop=True,
             )
-            tint = psum.tile([P, BANK], F32, name="pb", tag="pb")
+            tint = psum.tile([P, BANK], F32, name="bank")
             nc.tensor.matmul_mx(
                 out=tint[:],
                 lhsT=wd_dealt[:, P * i : P * (i + 1)].bitcast(FP8X4),
@@ -267,11 +273,15 @@ def tile_list_tattoo_fading_score_kernel(
             later[i, lo] = ring.tile([P, hi - lo], F32, name="later", align_bytes=64)
             nc.vector.tensor_copy(later[i, lo][:], ink[i][:].indirect(pos2_sb[:, lo // 16 : hi // 16]))
 
-        def difference(i, lo, hi):
+        earlier = {}
+
+        def pick_earlier(i, lo, hi):
+            earlier[i, lo] = ring.tile([P, hi - lo], F32, name="earlier", align_bytes=64)
+            nc.vector.tensor_copy(earlier[i, lo][:], ink[i][:].indirect(pos1_sb[:, lo // 16 : hi // 16]))
+
+        def difference(engine, i, lo, hi):
             g, t = divmod(i, PACK)
-            nc.vector.tensor_tensor(
-                y[g][:, t, lo:hi], ink[i][:].indirect(pos1_sb[:, lo // 16 : hi // 16]), later[i, lo][:], ALU.subtract
-            )
+            engine.tensor_tensor(y[g][:, t, lo:hi], earlier[i, lo][:], later[i, lo][:], ALU.subtract)
             rows = out_0[512 * g : 512 * (g + 1), :].rearrange("(p t) j -> p t j", t=PACK)
             nc.sync.dma_start(rows[:, t, lo:hi], y[g][:, t, lo:hi])
 
@@ -280,8 +290,8 @@ def tile_list_tattoo_fading_score_kernel(
         def round_y(copy, g, hf):
             y_bf[g, hf] = held([P, CHUNK, PACK], BF16, "y_bf%d%d" % (g, hf))
             copy(
-                y_bf[g, hf][:].rearrange("p (c i) t -> p c t i", i=4),
-                y[g][:, :, CHUNK * hf : CHUNK * (hf + 1)].rearrange("p t (c i) -> p c t i", i=4),
+                y_bf[g, hf][:].rearrange("p (c i) t -> p c t i", i=2),
+                y[g][:, :, CHUNK * hf : CHUNK * (hf + 1)].rearrange("p t (c i) -> p c t i", i=2),
             )
 
         def quantise_y(g, hf):
@@ -303,27 +313,31 @@ def tile_list_tattoo_fading_score_kernel(
             scores(i, hf)
         wc1 = round_and_deal(nc.scalar.copy, wc_raw[1], 0, PACK, "wc_bf1")
         for i in range(6):
-            scores(*halves[4 + 2 * i])
             pick_later(i, 0, PAIRS)
             if i == 1:
                 quantise_weight(wc1, wc_codes[1], wc_scales[1], 0, PACK)
-            scores(*halves[5 + 2 * i])
-            difference(i, 0, PAIRS)
-            if i == 3:
-                round_y(nc.scalar.copy, 0, 0)
-                round_y(nc.scalar.copy, 0, 1)
             if i == 5:
                 quantise_y(0, 0)
                 quantise_y(0, 1)
                 store_scales(0)
+            pick_earlier(i, 0, PAIRS)
+            difference(nc.gpsimd, i, 0, PAIRS)
+            scores(*halves[4 + 2 * i])
+            scores(*halves[5 + 2 * i])
+            if i == 3:
+                round_y(nc.scalar.copy, 0, 0)
+                round_y(nc.scalar.copy, 0, 1)
         pick_later(6, 0, PAIRS)
+        pick_earlier(6, 0, PAIRS)
         pick_later(7, 0, CHUNK)
-        difference(6, 0, PAIRS)
+        difference(nc.vector, 6, 0, PAIRS)
+        pick_earlier(7, 0, CHUNK)
         pick_later(7, CHUNK, PAIRS)
-        difference(7, 0, CHUNK)
+        difference(nc.vector, 7, 0, CHUNK)
         round_y(nc.scalar.copy, 1, 0)
-        difference(7, CHUNK, PAIRS)
-        round_y(nc.vector.tensor_copy, 1, 1)
+        pick_earlier(7, CHUNK, PAIRS)
+        difference(nc.vector, 7, CHUNK, PAIRS)
         quantise_y(1, 0)
+        round_y(nc.vector.tensor_copy, 1, 1)
         quantise_y(1, 1)
         store_scales(1)

@@ -29,7 +29,10 @@ def tile_list_tattoo_fading_score_kernel(
     with ExitStack() as ctx:
         keep = ctx.enter_context(tc.tile_pool(name="keep", bufs=1))
         ring = ctx.enter_context(tc.tile_pool(name="ring", bufs=3))
-        psum = ctx.enter_context(tc.psum_pool(name="psum", bufs=8))
+        psum = ctx.enter_context(tc.psum_pool(name="psum", bufs=1))
+
+        def bank_tile(n):
+            return psum.tile([P, BANK], F32, name="bank%d" % n)
 
         def held(shape, dtype, name):
             return keep.tile(shape, dtype, name=name, align_bytes=64)
@@ -49,7 +52,8 @@ def tile_list_tattoo_fading_score_kernel(
         wd_raw = held([P, N], U32, "wd_raw")
         wd_dealt = held([P, N], U32, "wd_dealt")
         gain_sb = held([P, PACK], F32, "gain_sb")
-        wa_raw = [held([P, PACK, H], F32, "wa_raw%d" % a) for a in range(2)]
+        wa_raw = held([P, PACK, H], F32, "wa_raw0")
+        wa_late = [held([P, PACK, H // 2], F32, "wa_late%d" % i) for i in range(2)]
         wc_raw = [held([P, PACK, BANK], F32, "wc_raw%d" % g) for g in range(2)]
         wa_codes = [held([P, H], U32, "wa_codes%d" % a) for a in range(2)]
         wa_scales = [held([P, H], U8, "wa_scales%d" % a) for a in range(2)]
@@ -94,8 +98,9 @@ def tile_list_tattoo_fading_score_kernel(
                 planes[32 * q : 32 * q + 4, :, :].bitcast(I32), staged[8 * q : 8 * q + 8, :].bitcast(I32)
             )
         load_table(1, T // 2, T)
-        for a in range(2):
-            nc.sync.dma_start(wa_raw[a][:], wa[512 * a : 512 * (a + 1), :].rearrange("(p j) c -> p j c", j=PACK))
+        nc.sync.dma_start(wa_raw[:], wa[0:512, :].rearrange("(p j) c -> p j c", j=PACK))
+        for i in range(2):
+            nc.sync.dma_start(wa_late[i][:], wa[512:1024, 256 * i : 256 * (i + 1)].rearrange("(p j) c -> p j c", j=PACK))
 
         def load_wc(g):
             nc.sync.dma_start(wc_raw[g][:], wc[:, BANK * g : BANK * (g + 1)].rearrange("(p j) c -> p j c", j=PACK))
@@ -120,7 +125,7 @@ def tile_list_tattoo_fading_score_kernel(
             )
 
         bg = [held([P, PACK, BANK], F32, "bg%d" % hf) for hf in range(2)]
-        b_banks = [[psum.tile([P, BANK], F32, name="bank") for t in range(PACK)] for hf in range(2)]
+        b_banks = [[bank_tile(PACK * hf + t) for t in range(PACK)] for hf in range(2)]
         for a in range(2):
             for hf in range(2):
                 cols = slice(BANK * hf, BANK * (hf + 1))
@@ -135,7 +140,7 @@ def tile_list_tattoo_fading_score_kernel(
                         stop=(a == 1),
                     )
         for hf in range(2):
-            for t in range(PACK - 2 * hf):
+            for t in range(PACK):
                 nc.scalar.activation(bg[hf][:, t, :], b_banks[hf][t][:], ACT.Copy, scale=gain_sb[:, t : t + 1])
 
         def round_and_deal(copy, raw, first, count, name):
@@ -170,16 +175,25 @@ def tile_list_tattoo_fading_score_kernel(
                     stop=(a == 1 and i == 1),
                 )
 
-        wa0 = round_and_deal(nc.vector.tensor_copy, wa_raw[0], 0, PACK, "wa_bf0")
+        wa0 = round_and_deal(nc.vector.tensor_copy, wa_raw, 0, PACK, "wa_bf0")
         quantise_weight(wa0, wa_codes[0], wa_scales[0], 0, PACK)
         a_banks = {}
         for c in range(2):
             for pair in range(2):
-                a_banks[c, pair] = psum.tile([P, BANK], F32, name="bank")
+                a_banks[c, pair] = bank_tile(2 * (c % 2) + pair)
                 a_passes(a_banks[c, pair], c, pair, 0)
+        wa1 = held([P, PACK, P, PACK], BF16, "wa_bf1")
+        wa1_out = wa1[:].rearrange("p (u e) m j -> p u m j e", e=2)
+        nc.vector.tensor_copy(wa1_out[:, :, 0:64, :, :], wa_late[0][:].rearrange("p j (m u e) -> p u m j e", u=2, e=2))
         for pair in range(2):
-            wa1 = round_and_deal(nc.vector.tensor_copy, wa_raw[1], 2 * pair, 2, "wa_bf1%d" % pair)
-            quantise_weight(wa1, wa_codes[1], wa_scales[1], 2 * pair, 2)
+            nc.vector.tensor_copy(
+                wa1_out[:, pair, 64:128, :, :], wa_late[1][:].rearrange("p j (m u e) -> p u m j e", u=2, e=2)[:, pair, :, :, :]
+            )
+        for pair in range(2):
+            cols = slice(2 * P * pair, 2 * P * (pair + 1))
+            quantise(
+                wa1[:, 2 * pair : 2 * pair + 2, :, :].rearrange("p t m j -> p (t m j)"), wa_codes[1][:, cols], wa_scales[1][:, cols]
+            )
 
         damp = {}
 
@@ -187,13 +201,13 @@ def tile_list_tattoo_fading_score_kernel(
             size = ring.tile([P, PACK, CHUNK], F32, name="size", bufs=2, align_bytes=64)
             for pair in range(2):
                 if (c, pair) not in a_banks:
-                    a_banks[c, pair] = psum.tile([P, BANK], F32, name="bank")
+                    a_banks[c, pair] = bank_tile(2 * (c % 2) + pair)
                     a_passes(a_banks[c, pair], c, pair, 0)
                 a_passes(a_banks[c, pair], c, pair, 1)
                 nc.scalar.activation(
                     size[:, 2 * pair : 2 * pair + 2, :].rearrange("p t m -> p (t m)"), a_banks[c, pair][:], ACT.Abs
                 )
-            damp[c] = ring.tile([P, PACK, CHUNK], F32, name="damp", bufs=2, align_bytes=64)
+            damp[c] = ring.tile([P, PACK, CHUNK], F32, name="damp", align_bytes=64)
             nc.scalar.activation(
                 damp[c][:].rearrange("p t m -> p (t m)"), size[:].rearrange("p t m -> p (t m)"), ACT.Exp, scale=-1.0
             )
@@ -220,8 +234,6 @@ def tile_list_tattoo_fading_score_kernel(
         features(0)
         quantise_weight(wc0, wc_codes[0], wc_scales[0], 0, PACK)
         quantise_h(0)
-        for t in range(2, PACK):
-            nc.vector.tensor_scalar_mul(bg[1][:, t, :], b_banks[1][t][:], gain_sb[:, t : t + 1])
         nc.vector.tensor_copy(
             wd_dealt[:].bitcast(I32).rearrange("p (g u e m) -> p g u m e", g=2, u=2, e=2),
             wd_raw[:].bitcast(I32).rearrange("p (g m u e) -> p g u m e", g=2, u=2, e=2),
@@ -231,19 +243,19 @@ def tile_list_tattoo_fading_score_kernel(
         features(2)
         quantise_h(2)
         features(3)
-        quantise_h(3)
 
         ink = {}
         y = [held([P, PACK, PAIRS], F32, "y%d" % g) for g in range(2)]
         y_codes = [held([P, PAIRS], U32, "y_codes%d" % g) for g in range(2)]
         y_scales = [held([P, PAIRS], U8, "y_scales%d" % g) for g in range(2)]
 
-        def scores(i, hf):
+        def scores(unit):
+            i, hf = halves[unit]
             g, t = divmod(i, PACK)
             if hf == 0:
                 ink[i] = ring.tile([P, S], F32, name="ink", bufs=4, align_bytes=64)
             cols = slice(BANK * hf, BANK * (hf + 1))
-            dark = psum.tile([P, BANK], F32, name="bank")
+            dark = bank_tile((2 * unit + 4) % 8)
             nc.tensor.matmul_mx(
                 out=dark[:],
                 lhsT=wc_codes[g][:, P * t : P * (t + 1)].bitcast(FP8X4),
@@ -253,7 +265,7 @@ def tile_list_tattoo_fading_score_kernel(
                 start=True,
                 stop=True,
             )
-            tint = psum.tile([P, BANK], F32, name="bank")
+            tint = bank_tile((2 * unit + 5) % 8)
             nc.tensor.matmul_mx(
                 out=tint[:],
                 lhsT=wd_dealt[:, P * i : P * (i + 1)].bitcast(FP8X4),
@@ -273,15 +285,11 @@ def tile_list_tattoo_fading_score_kernel(
             later[i, lo] = ring.tile([P, hi - lo], F32, name="later", align_bytes=64)
             nc.vector.tensor_copy(later[i, lo][:], ink[i][:].indirect(pos2_sb[:, lo // 16 : hi // 16]))
 
-        earlier = {}
-
-        def pick_earlier(i, lo, hi):
-            earlier[i, lo] = ring.tile([P, hi - lo], F32, name="earlier", align_bytes=64)
-            nc.vector.tensor_copy(earlier[i, lo][:], ink[i][:].indirect(pos1_sb[:, lo // 16 : hi // 16]))
-
-        def difference(engine, i, lo, hi):
+        def difference(i, lo, hi):
             g, t = divmod(i, PACK)
-            engine.tensor_tensor(y[g][:, t, lo:hi], earlier[i, lo][:], later[i, lo][:], ALU.subtract)
+            nc.vector.tensor_tensor(
+                y[g][:, t, lo:hi], ink[i][:].indirect(pos1_sb[:, lo // 16 : hi // 16]), later[i, lo][:], ALU.subtract
+            )
             rows = out_0[512 * g : 512 * (g + 1), :].rearrange("(p t) j -> p t j", t=PACK)
             nc.sync.dma_start(rows[:, t, lo:hi], y[g][:, t, lo:hi])
 
@@ -309,35 +317,33 @@ def tile_list_tattoo_fading_score_kernel(
 
         halves = [(i, 0) for i in range(3)] + [(i, 1) for i in range(3)]
         halves = halves + [(i, hf) for i in range(3, 8) for hf in range(2)]
-        for i, hf in halves[:4]:
-            scores(i, hf)
+        scores(0)
+        quantise_h(3)
+        for unit in range(1, 4):
+            scores(unit)
         wc1 = round_and_deal(nc.scalar.copy, wc_raw[1], 0, PACK, "wc_bf1")
         for i in range(6):
+            scores(4 + 2 * i)
             pick_later(i, 0, PAIRS)
             if i == 1:
                 quantise_weight(wc1, wc_codes[1], wc_scales[1], 0, PACK)
+            scores(5 + 2 * i)
+            difference(i, 0, PAIRS)
+            if i == 3:
+                round_y(nc.scalar.copy, 0, 0)
+                round_y(nc.scalar.copy, 0, 1)
             if i == 5:
                 quantise_y(0, 0)
                 quantise_y(0, 1)
                 store_scales(0)
-            pick_earlier(i, 0, PAIRS)
-            difference(nc.gpsimd, i, 0, PAIRS)
-            scores(*halves[4 + 2 * i])
-            scores(*halves[5 + 2 * i])
-            if i == 3:
-                round_y(nc.scalar.copy, 0, 0)
-                round_y(nc.scalar.copy, 0, 1)
         pick_later(6, 0, PAIRS)
-        pick_earlier(6, 0, PAIRS)
         pick_later(7, 0, CHUNK)
-        difference(nc.vector, 6, 0, PAIRS)
-        pick_earlier(7, 0, CHUNK)
+        difference(6, 0, PAIRS)
         pick_later(7, CHUNK, PAIRS)
-        difference(nc.vector, 7, 0, CHUNK)
+        difference(7, 0, CHUNK)
         round_y(nc.scalar.copy, 1, 0)
-        pick_earlier(7, CHUNK, PAIRS)
-        difference(nc.vector, 7, CHUNK, PAIRS)
-        quantise_y(1, 0)
+        difference(7, CHUNK, PAIRS)
         round_y(nc.vector.tensor_copy, 1, 1)
+        quantise_y(1, 0)
         quantise_y(1, 1)
         store_scales(1)

from contextlib import ExitStack

import concourse.mybir as mybir

K, H, N, T, S, PAIRS = 1024, 512, 1024, 4096, 1024, 512
FLOPS = 2 * 2 * K * H * S + 2 * 2 * H * N * S

F32 = mybir.dt.float32
BF16 = mybir.dt.bfloat16
I32 = mybir.dt.int32
U32 = mybir.dt.uint32
U16 = mybir.dt.uint16
U8 = mybir.dt.uint8
FP8X4 = mybir.dt.float8_e4m3fn_x4
FP4X4 = mybir.dt.float4_e2m1fn_x4
ALU = mybir.AluOpType
ACT = mybir.ActivationFunctionType

P = 128
PACK = 4
BANK = 512
CHUNK = 256


def tile_list_tattoo_fading_score_kernel(
    tc, tab_words, tab_scales, offs, pos1, pos2, wa, wb_words, wb_scales, gain, wc, wd_words, wd_scales, out_0, out_1, out_2
):
    nc = tc.nc
    with ExitStack() as ctx:
        keep = ctx.enter_context(tc.tile_pool(name="keep", bufs=1))
        ring = ctx.enter_context(tc.tile_pool(name="ring", bufs=3))
        psum = ctx.enter_context(tc.psum_pool(name="psum", bufs=1))

        def bank_tile(n):
            return psum.tile([P, BANK], F32, name="bank%d" % n)

        def held(shape, dtype, name):
            return keep.tile(shape, dtype, name=name, align_bytes=64)

        offs_sb = keep.tile([P, S // 16], U16, name="offs_sb")
        pos1_sb = keep.tile([P, PAIRS // 16], U16, name="pos1_sb")
        pos2_sb = keep.tile([P, PAIRS // 16], U16, name="pos2_sb")
        tab_sb = [held([P, T], U32, "tab_sb%d" % a) for a in range(2)]
        tabsc_raw = held([P, T], U8, "tabsc_raw")
        tabsc_picked = held([P, S], U8, "tabsc_picked")
        staged = held([P, S + 2 * BANK], U8, "staged")
        planes = held([P, 2, S + 2 * BANK], U8, "planes")
        v_words = [held([P, S], U32, "v_words%d" % a) for a in range(2)]
        wb_raw = held([P, 2, 2 * H], U8, "wb_raw")
        wb_dealt = held([P, 2, 2 * H], U8, "wb_dealt")
        wsc_raw = held([P, 2, BANK], U8, "wsc_raw")
        wd_raw = held([P, N], U32, "wd_raw")
        wd_dealt = held([P, N], U32, "wd_dealt")
        gain_sb = held([P, PACK], F32, "gain_sb")
        wa_raw = held([P, PACK, H], F32, "wa_raw0")
        wa_late = [held([P, PACK, H // 2], F32, "wa_late%d" % i) for i in range(2)]
        wc_raw = [held([P, PACK, BANK], F32, "wc_raw%d" % g) for g in range(2)]
        wa_codes = [held([P, H], U32, "wa_codes%d" % a) for a in range(2)]
        wa_scales = [held([P, H], U8, "wa_scales%d" % a) for a in range(2)]
        wc_codes = [held([P, BANK], U32, "wc_codes%d" % g) for g in range(2)]
        wc_scales = [held([P, BANK], U8, "wc_scales%d" % g) for g in range(2)]
        h_codes = held([P, S], U32, "h_codes")
        h_scales = held([P, S], U8, "h_scales")
        warm = held([P, 8], F32, "warm")

        nc.sync.dma_start(offs_sb[:], offs)
        nc.sync.dma_start(tabsc_raw[0:32, :].bitcast(I32), tab_scales.rearrange("a q t -> q a t").bitcast(I32))
        nc.sync.dma_start(wsc_raw[0:32, 0, :].bitcast(I32), wb_scales.rearrange("a q c -> q a c").bitcast(I32))
        nc.sync.dma_start(wsc_raw[0:32, 1, :].bitcast(I32), wd_scales[0].rearrange("q (g c) -> (q g) c", g=2).bitcast(I32))
        for lo, hi in ((32, 64), (64, P)):
            nc.vector.memset(tabsc_raw[lo:hi, :].bitcast(I32), 0)
            nc.vector.memset(wsc_raw[lo:hi, :, :].rearrange("p a c -> p (a c)").bitcast(I32), 0)
        nc.vector.memset(planes[:].rearrange("p a c -> p (a c)").bitcast(I32), 0)
        nc.vector.memset(warm[:], 0.0)
        nc.scalar.activation(warm[:, 4:5], warm[:, 0:1], ACT.Exp)

        def load_table(a, lo, hi):
            words = tab_words[a].rearrange("p t i -> p (t i)").bitcast(I32)
            nc.sync.dma_start(tab_sb[a][:, lo:hi].bitcast(I32), words[:, lo:hi])

        nc.sync.dma_start(wb_raw[:, 0, :].bitcast(I32), wb_words[0].bitcast(I32))
        load_table(0, 0, T)
        nc.sync.dma_start(gain_sb[:], gain.rearrange("(p t) -> p t", t=PACK))
        nc.sync.dma_start(pos1_sb[:], pos1)
        nc.sync.dma_start(pos2_sb[:], pos2)
        nc.sync.dma_start(wb_raw[:, 1, :].bitcast(I32), wb_words[1].bitcast(I32))
        for i in range(4):
            load_table(1, i * T // 8, (i + 1) * T // 8)

        nc.vector.tensor_copy(
            staged[:, S:].rearrange("p (w t m) -> p w t m", w=2, t=PACK),
            wsc_raw[:].rearrange("p w (m t) -> p w t m", t=PACK),
        )
        nc.vector.tensor_copy(tabsc_picked[:], tabsc_raw[:].indirect(offs_sb[:]))
        nc.vector.tensor_copy(staged[0:32, 0:S].bitcast(I32), tabsc_picked[0:32, :].bitcast(I32))
        for q in range(4):
            nc.sync.dma_start(
                planes[32 * q : 32 * q + 4, :, :].bitcast(I32), staged[8 * q : 8 * q + 8, :].bitcast(I32)
            )
        load_table(1, T // 2, T)
        nc.sync.dma_start(wa_raw[:], wa[0:512, :].rearrange("(p j) c -> p j c", j=PACK))
        for i in range(2):
            nc.sync.dma_start(wa_late[i][:], wa[512:1024, 256 * i : 256 * (i + 1)].rearrange("(p j) c -> p j c", j=PACK))

        def load_wc(g):
            nc.sync.dma_start(wc_raw[g][:], wc[:, BANK * g : BANK * (g + 1)].rearrange("(p j) c -> p j c", j=PACK))

        load_wc(0)
        nc.sync.dma_start(wd_raw[:].bitcast(I32), wd_words[0].rearrange("p c i -> p (c i)").bitcast(I32))
        load_wc(1)

        def deal_wb(a):
            nc.vector.tensor_copy(
                wb_dealt[:, a, :].bitcast(U16).rearrange("p (t m) -> p t m", t=PACK),
                wb_raw[:, a, :].bitcast(U16).rearrange("p (m t) -> p t m", t=PACK),
            )

        deal_wb(0)
        nc.vector.tensor_copy(v_words[0][:], tab_sb[0][:].indirect(offs_sb[:]))
        deal_wb(1)
        for hf in range(2):
            nc.vector.tensor_copy(
                v_words[1][:, BANK * hf : BANK * (hf + 1)],
                tab_sb[1][:].indirect(offs_sb[:, 32 * hf : 32 * (hf + 1)]),
            )

        bg = [held([P, PACK, BANK], F32, "bg%d" % hf) for hf in range(2)]
        b_banks = [[bank_tile(PACK * hf + t) for t in range(PACK)] for hf in range(2)]
        for a in range(2):
            for hf in range(2):
                cols = slice(BANK * hf, BANK * (hf + 1))
                for t in range(PACK):
                    nc.tensor.matmul_mx(
                        out=b_banks[hf][t][:],
                        lhsT=wb_dealt[:, a, 2 * P * t : 2 * P * (t + 1)].bitcast(FP4X4),
                        lhsT_scale=planes[:, a, S + P * t : S + P * (t + 1)],
                        rhs=v_words[a][:, cols].bitcast(FP8X4),
                        rhs_scale=planes[:, a, cols],
                        start=(a == 0),
                        stop=(a == 1),
                    )
        for hf in range(2):
            for t in range(PACK):
                nc.scalar.activation(bg[hf][:, t, :], b_banks[hf][t][:], ACT.Copy, scale=gain_sb[:, t : t + 1])

        def round_and_deal(copy, raw, first, count, name):
            if name == "wc_bf1":
                dealt = ring.tile([P, count, P, PACK], BF16, name=name, tag="size", bufs=2, align_bytes=64)
            else:
                dealt = held([P, count, P, PACK], BF16, name)
            copy(
                dealt[:].rearrange("p (u e) m j -> p u m j e", e=2),
                raw[:].rearrange("p j (m u e) -> p u m j e", u=2, e=2)[:, first // 2 : (first + count) // 2, :, :, :],
            )
            return dealt

        def quantise(dealt, codes, scales):
            nc.vector.quantize_mx(out=codes.bitcast(FP8X4), scales=scales, in_=dealt)

        def quantise_weight(dealt, codes, scales, first, count):
            cols = slice(P * first, P * (first + count))
            quantise(dealt[:].rearrange("p t m j -> p (t m j)"), codes[:, cols], scales[:, cols])

        def a_passes(bank, c, pair, a):
            cols = slice(CHUNK * c, CHUNK * (c + 1))
            for i in range(2):
                t = 2 * pair + i
                nc.tensor.matmul_mx(
                    out=bank[:, CHUNK * i : CHUNK * (i + 1)],
                    lhsT=wa_codes[a][:, P * t : P * (t + 1)].bitcast(FP8X4),
                    lhsT_scale=wa_scales[a][:, P * t : P * (t + 1)],
                    rhs=v_words[a][:, cols].bitcast(FP8X4),
                    rhs_scale=planes[:, a, cols],
                    start=(a == 0 and i == 0),
                    stop=(a == 1 and i == 1),
                )

        wa0 = round_and_deal(nc.vector.tensor_copy, wa_raw, 0, PACK, "wa_bf0")
        quantise_weight(wa0, wa_codes[0], wa_scales[0], 0, PACK)
        a_banks = {}
        for c in range(2):
            for pair in range(2):
                a_banks[c, pair] = bank_tile(2 * (c % 2) + pair)
                a_passes(a_banks[c, pair], c, pair, 0)
        wa1 = held([P, PACK, P, PACK], BF16, "wa_bf1")
        wa1_out = wa1[:].rearrange("p (u e) m j -> p u m j e", e=2)
        nc.vector.tensor_copy(wa1_out[:, :, 0:64, :, :], wa_late[0][:].rearrange("p j (m u e) -> p u m j e", u=2, e=2))
        for pair in range(2):
            nc.vector.tensor_copy(
                wa1_out[:, pair, 64:128, :, :], wa_late[1][:].rearrange("p j (m u e) -> p u m j e", u=2, e=2)[:, pair, :, :, :]
            )
        for pair in range(2):
            cols = slice(2 * P * pair, 2 * P * (pair + 1))
            quantise(
                wa1[:, 2 * pair : 2 * pair + 2, :, :].rearrange("p t m j -> p (t m j)"), wa_codes[1][:, cols], wa_scales[1][:, cols]
            )

        damp = {}

        def damping(c):
            size = ring.tile([P, PACK, CHUNK], F32, name="size", bufs=2, align_bytes=64)
            for pair in range(2):
                if (c, pair) not in a_banks:
                    a_banks[c, pair] = bank_tile(2 * (c % 2) + pair)
                    a_passes(a_banks[c, pair], c, pair, 0)
                a_passes(a_banks[c, pair], c, pair, 1)
                nc.scalar.activation(
                    size[:, 2 * pair : 2 * pair + 2, :].rearrange("p t m -> p (t m)"), a_banks[c, pair][:], ACT.Abs
                )
            damp[c] = ring.tile([P, PACK, CHUNK], F32, name="damp", align_bytes=64)
            nc.scalar.activation(
                damp[c][:].rearrange("p t m -> p (t m)"), size[:].rearrange("p t m -> p (t m)"), ACT.Exp, scale=-1.0
            )

        h_bf = {}

        def features(c):
            h_bf[c] = ring.tile([P, CHUNK, PACK], BF16, name="h_bf", align_bytes=64)
            lo = CHUNK * (c % 2)
            nc.vector.tensor_tensor(
                h_bf[c][:].rearrange("p (c i) t -> p c t i", i=2),
                damp[c][:].rearrange("p t (c i) -> p c t i", i=2),
                bg[c // 2][:, :, lo : lo + CHUNK].rearrange("p t (c i) -> p c t i", i=2),
                ALU.mult,
            )

        def quantise_h(c):
            cols = slice(CHUNK * c, CHUNK * (c + 1))
            quantise(h_bf[c][:].rearrange("p m t -> p (m t)"), h_codes[:, cols], h_scales[:, cols])

        for c in range(4):
            damping(c)
        wc0 = round_and_deal(nc.vector.tensor_copy, wc_raw[0], 0, PACK, "wc_bf0")
        features(0)
        quantise_weight(wc0, wc_codes[0], wc_scales[0], 0, PACK)
        quantise_h(0)
        nc.vector.tensor_copy(
            wd_dealt[:].bitcast(I32).rearrange("p (g u e m) -> p g u m e", g=2, u=2, e=2),
            wd_raw[:].bitcast(I32).rearrange("p (g m u e) -> p g u m e", g=2, u=2, e=2),
        )
        features(1)
        quantise_h(1)
        features(2)
        quantise_h(2)
        features(3)

        ink = {}
        y = [held([P, PACK, PAIRS], F32, "y%d" % g) for g in range(2)]
        y_codes = [held([P, PAIRS], U32, "y_codes%d" % g) for g in range(2)]
        y_scales = [held([P, PAIRS], U8, "y_scales%d" % g) for g in range(2)]

        def scores(unit):
            i, hf = halves[unit]
            g, t = divmod(i, PACK)
            if hf == 0:
                ink[i] = ring.tile([P, S], F32, name="ink", bufs=4, align_bytes=64)
            cols = slice(BANK * hf, BANK * (hf + 1))
            dark = bank_tile((2 * unit + 4) % 8)
            nc.tensor.matmul_mx(
                out=dark[:],
                lhsT=wc_codes[g][:, P * t : P * (t + 1)].bitcast(FP8X4),
                lhsT_scale=wc_scales[g][:, P * t : P * (t + 1)],
                rhs=h_codes[:, cols].bitcast(FP8X4),
                rhs_scale=h_scales[:, cols],
                start=True,
                stop=True,
            )
            tint = bank_tile((2 * unit + 5) % 8)
            nc.tensor.matmul_mx(
                out=tint[:],
                lhsT=wd_dealt[:, P * i : P * (i + 1)].bitcast(FP8X4),
                lhsT_scale=planes[:, g, S + BANK + P * t : S + BANK + P * (t + 1)],
                rhs=h_codes[:, cols].bitcast(FP8X4),
                rhs_scale=h_scales[:, cols],
                start=True,
                stop=True,
            )
            dark_sb = ring.tile([P, BANK], F32, name="dark_sb", bufs=4, align_bytes=64)
            nc.scalar.copy(dark_sb[:], dark[:])
            nc.vector.tensor_tensor(ink[i][:, cols], tint[:], dark_sb[:], ALU.max)

        later = {}

        def pick_later(i, lo, hi):
            later[i, lo] = ring.tile([P, hi - lo], F32, name="later", align_bytes=64)
            nc.vector.tensor_copy(later[i, lo][:], ink[i][:].indirect(pos2_sb[:, lo // 16 : hi // 16]))

        def difference(i, lo, hi):
            g, t = divmod(i, PACK)
            nc.vector.tensor_tensor(
                y[g][:, t, lo:hi], ink[i][:].indirect(pos1_sb[:, lo // 16 : hi // 16]), later[i, lo][:], ALU.subtract
            )
            rows = out_0[512 * g : 512 * (g + 1), :].rearrange("(p t) j -> p t j", t=PACK)
            nc.sync.dma_start(rows[:, t, lo:hi], y[g][:, t, lo:hi])

        y_bf = {}

        def round_y(copy, g, hf):
            y_bf[g, hf] = held([P, CHUNK, PACK], BF16, "y_bf%d%d" % (g, hf))
            copy(
                y_bf[g, hf][:].rearrange("p (c i) t -> p c t i", i=2),
                y[g][:, :, CHUNK * hf : CHUNK * (hf + 1)].rearrange("p t (c i) -> p c t i", i=2),
            )

        def quantise_y(g, hf):
            cols = slice(CHUNK * hf, CHUNK * (hf + 1))
            quantise(y_bf[g, hf][:].rearrange("p m t -> p (m t)"), y_codes[g][:, cols], y_scales[g][:, cols])
            words = out_1[g].rearrange("p m t -> p (m t)").bitcast(I32)
            nc.sync.dma_start(words[:, cols], y_codes[g][:, cols].bitcast(I32))

        def store_scales(g):
            for q in range(4):
                queue = nc.scalar if q % 2 else nc.sync
                queue.dma_start(
                    out_2[g, 4 * q : 4 * q + 4, :].bitcast(I32), y_scales[g][32 * q : 32 * q + 4, :].bitcast(I32)
                )

        halves = [(i, 0) for i in range(3)] + [(i, 1) for i in range(3)]
        halves = halves + [(i, hf) for i in range(3, 8) for hf in range(2)]
        scores(0)
        quantise_h(3)
        for unit in range(1, 4):
            scores(unit)
        wc1 = round_and_deal(nc.scalar.copy, wc_raw[1], 0, PACK, "wc_bf1")
        for i in range(6):
            scores(4 + 2 * i)
            pick_later(i, 0, PAIRS)
            if i == 1:
                quantise_weight(wc1, wc_codes[1], wc_scales[1], 0, PACK)
            scores(5 + 2 * i)
            difference(i, 0, PAIRS)
            if i == 3:
                round_y(nc.scalar.copy, 0, 0)
                round_y(nc.scalar.copy, 0, 1)
            if i == 5:
                quantise_y(0, 0)
                quantise_y(0, 1)
                store_scales(0)
        pick_later(6, 0, PAIRS)
        pick_later(7, 0, CHUNK)
        difference(6, 0, PAIRS)
        pick_later(7, CHUNK, PAIRS)
        difference(7, 0, CHUNK)
        round_y(nc.scalar.copy, 1, 0)
        difference(7, CHUNK, PAIRS)
        round_y(nc.vector.tensor_copy, 1, 1)
        quantise_y(1, 0)
        quantise_y(1, 1)
        store_scales(1)
